import numpy as np
import ml_dtypes


def mxq(x, axis, fmt="e4m3"):
    dtype, down = {"e4m3": (ml_dtypes.float8_e4m3fn, 7), "e5m2": (ml_dtypes.float8_e5m2, 14)}[fmt]
    v = np.moveaxis(np.asarray(x, np.float32).astype(ml_dtypes.bfloat16).astype(np.float64), axis, -1)
    blocks = v.reshape(v.shape[:-1] + (-1, 32))
    amax = np.abs(blocks).max(-1, keepdims=True)
    byte = np.maximum(np.where(amax > 0, np.frexp(amax)[1] - 1 + 127, 0) - down, 1)
    scale = np.exp2(byte - 127.0)
    codes = (blocks / scale).astype(np.float32).astype(dtype).astype(np.float64)
    return np.moveaxis((codes * scale).reshape(v.shape), -1, axis)


WIDE = False


def mx_kscale(k):
    if not WIDE:
        return np.ones(k)
    levels = np.array([30, -30])
    if k % 512:
        return np.exp2(np.random.permutation(np.resize(levels, k // 32))).repeat(32)
    a = np.empty((k // 512, 16))
    for p in range(k // 512):
        a[p, :8] = np.random.permutation(np.resize(levels, 8))
        for g in range(8):
            far = levels[np.abs(levels - a[p, g]) >= 10]
            a[p, g + 8] = far[np.random.randint(len(far))]
    return np.exp2(a.ravel()).repeat(32)


def f64(x):
    return np.asarray(x).astype(np.float64)


def striped(idx):
    return np.tile(np.asarray(idx).reshape(-1, 16).T, (8, 1)).astype(np.uint16)


def unstriped(offs):
    return offs[:16].T.reshape(-1).astype(np.int64)


E2M1 = np.array([0.0, 0.5, 1.0, 1.5, 2.0, 3.0, 4.0, 6.0, -0.0, -0.5, -1.0, -1.5, -2.0, -3.0, -4.0, -6.0])


def pack_weight(w, fmt):
    k, n = w.shape
    w = f64(np.asarray(w, np.float32).astype(ml_dtypes.bfloat16)).reshape(k // 32, 32, n)
    amax = np.abs(w).max(1)
    if fmt in ("e4m3", "e5m2"):
        byte = np.frexp(amax)[1] - 1 + 127 - (7 if fmt == "e4m3" else 14)
    else:
        mant, ex = np.frexp(amax / 6.0)
        byte = np.where(mant > 0.5, ex, ex - 1) + 127
    byte = np.clip(np.where(amax > 0, byte, 1), 1, 254)
    scaled = (w * np.exp2(127.0 - byte)[:, None, :]).reshape(k, n).astype(np.float32)
    by_word = np.ascontiguousarray(scaled.reshape(k // 512, 128, 4, n).transpose(0, 1, 3, 2))
    if fmt in ("e4m3", "e5m2"):
        words = by_word.astype(ml_dtypes.float8_e4m3fn if fmt == "e4m3" else ml_dtypes.float8_e5m2).view(np.uint8)
    else:
        c = by_word.astype(ml_dtypes.float4_e2m1fn).view(np.uint8) & 0xF
        words = (c[..., 0::2] | (c[..., 1::2] << 4)).reshape(k // 512, 128, 2 * n)
    return np.ascontiguousarray(words), np.ascontiguousarray(byte.astype(np.uint8).reshape(k // 512, 16, n))


def unpack_weight(words, scales, fmt):
    g, _, n = scales.shape
    words = np.ascontiguousarray(words).reshape(g, 128, n, -1)
    if fmt in ("e4m3", "e5m2"):
        vals = words.view(ml_dtypes.float8_e4m3fn if fmt == "e4m3" else ml_dtypes.float8_e5m2).astype(np.float64)
    else:
        nib = np.empty((g, 128, n, 4), np.uint8)
        nib[..., 0::2] = words & 0xF
        nib[..., 1::2] = words >> 4
        vals = E2M1[nib]
    vals = vals * np.repeat(np.exp2(scales.astype(np.float64) - 127.0), 8, axis=1)[..., None]
    return vals.transpose(0, 1, 3, 2).reshape(g * 512, n)


def bf(x):
    return np.asarray(x, np.float32).astype(ml_dtypes.bfloat16)


def planes(Y):
    r, m = Y.shape
    b = f64(bf(Y)).reshape(r // 32, 32, m)
    amax = np.abs(b).max(1)
    byte = np.clip(np.where(amax > 0, np.frexp(amax)[1] - 1 + 127 - 7, 1), 1, 254)
    codes = (b * np.exp2(127.0 - byte)[:, None, :]).reshape(r, m).astype(np.float32).astype(ml_dtypes.float8_e4m3fn).view(np.uint8)
    words = codes.reshape(r // 512, 128, 4, m).transpose(0, 1, 3, 2)
    return np.ascontiguousarray(words), np.ascontiguousarray(byte.astype(np.uint8).reshape(r // 512, 16, m))


K, T, J, R, N, Q = 512, 1024, 256, 512, 512, 64


def setup_inputs():
    n = np.random.standard_normal
    idx = np.random.permutation(T)[:J]
    fk = mx_kscale(K)
    fr = mx_kscale(R)
    xtp = pack_weight(n((K, T)) / fk[:, None], "e5m2")
    wp = pack_weight(n((K, R)) * 1 / np.sqrt(K) * fk[:, None] * fr, "e4m3")
    wbp = pack_weight(n((R, N)) * 1 / np.sqrt(R) / fr[:, None], "e2m1")
    return {
        "xt_words": xtp[0],
        "xt_scales": xtp[1],
        "w_words": wp[0],
        "w_scales": wp[1],
        "us": (np.random.uniform(0.5, 2.0, (R, 1)) * fr[:, None]).astype(np.float32),
        "wb_words": wbp[0],
        "wb_scales": wbp[1],
        "rw": (np.random.uniform(0.5, 2.0, (1, J))).astype(np.float32),
        "qw": (np.random.uniform(0.5, 2.0, (1, Q))).astype(np.float32),
        "offs": striped(idx),
    }


def reference(xt_words, xt_scales, w_words, w_scales, us, wb_words, wb_scales, rw, qw, offs):
    idx = unstriped(offs)
    xtu = unpack_weight(xt_words, xt_scales, "e5m2")
    wu = unpack_weight(w_words, w_scales, "e4m3")
    wbu = unpack_weight(wb_words, wb_scales, "e2m1")
    xtidxg = xtu[:, idx]
    a = wu.T @ xtidxg
    pk1 = np.max(np.abs(a), axis=1, keepdims=True)
    hid = a / pk1 * f64(us)
    hidq = mxq(hid, 0, "e5m2")
    p = wbu.T @ hidq
    y = (p * f64(rw)).reshape(N, Q, J // Q).sum(axis=2) * f64(qw)
    words, scales = planes(y)
    return y, words, scales

@@ -1,0 +1,206 @@
+from contextlib import ExitStack
+
+import concourse.mybir as mybir
+from concourse.masks import make_identity
+
+K, T, J, R, N, Q = 512, 1024, 256, 512, 512, 64
+FLOPS = 2 * K * R * J + 2 * R * N * J
+
+F32 = mybir.dt.float32
+BF16 = mybir.dt.bfloat16
+I32 = mybir.dt.int32
+U32 = mybir.dt.uint32
+U16 = mybir.dt.uint16
+U8 = mybir.dt.uint8
+E4M3 = mybir.dt.float8_e4m3fn_x4
+E5M2 = mybir.dt.float8_e5m2_x4
+E2M1 = mybir.dt.float4_e2m1fn_x4
+ALU = mybir.AluOpType
+AX = mybir.AxisListType
+
+P = 128
+PACK = 4
+SET = J // Q
+HALF = J // 2
+QH = Q // 2
+SCALAR_SLOTS = 64
+
+
+def load_scale_rows(queues, plane, rows):
+    for quad in range(4):
+        queues[quad].dma_start(
+            out=plane[32 * quad : 32 * quad + 4, :].bitcast(I32),
+            in_=rows[4 * quad : 4 * quad + 4, :].bitcast(I32),
+        )
+
+
+def deal_columns(nc, dealt, raw, run):
+    nc.vector.tensor_copy(
+        out=dealt.rearrange("p (t c i) -> p c t i", t=PACK, i=run),
+        in_=raw.rearrange("p (c i t) -> p c t i", t=PACK, i=run),
+    )
+
+
+def tile_list_picked_peakscaled_groupsums_pl_kernel(
+    tc, xt_words, xt_scales, w_words, w_scales, us, wb_words, wb_scales, rw, qw, offs, out_0, out_1, out_2
+):
+    nc = tc.nc
+    with ExitStack() as ctx:
+        sb = ctx.enter_context(tc.tile_pool(name="sb", bufs=1))
+        ps = ctx.enter_context(tc.psum_pool(name="ps", bufs=1))
+
+        offsets = sb.tile([P, J // 16], U16, name="offsets")
+        x_words = sb.tile([P, T], U32, name="x_words", align_bytes=64)
+        x_plane = sb.tile([P, T], U8, name="x_plane", align_bytes=64)
+        w_raw = sb.tile([P, R], U32, name="w_raw", align_bytes=64)
+        w_plane_raw = sb.tile([P, R], U8, name="w_plane_raw", align_bytes=64)
+        wb_raw = sb.tile([P, 2 * N], U8, name="wb_raw", align_bytes=64)
+        wb_plane_raw = sb.tile([P, N], U8, name="wb_plane_raw", align_bytes=64)
+        us_sb = sb.tile([P, PACK], F32, name="us_sb")
+        rw_sb = sb.tile([Q, SET], F32, name="rw_sb")
+        qw_sb = sb.tile([Q, 1], F32, name="qw_sb")
+
+        nc.gpsimd.memset(x_plane[:].bitcast(I32), 0)
+        nc.vector.memset(w_plane_raw[:].bitcast(I32), 0)
+        nc.vector.memset(wb_plane_raw[:].bitcast(I32), 0)
+
+        nc.sync.dma_start(offsets[:], offs)
+        nc.sync.dma_start(out=us_sb[:], in_=us.rearrange("(p t) o -> p (t o)", t=PACK))
+        nc.sync.dma_start(out=w_raw[:].bitcast(I32), in_=w_words[0].rearrange("p n t -> p (n t)").bitcast(I32))
+        load_scale_rows([nc.sync] * 4, x_plane, xt_scales[0])
+        nc.sync.dma_start(out=x_words[:].bitcast(I32), in_=xt_words[0].rearrange("p n t -> p (n t)").bitcast(I32))
+        load_scale_rows([nc.sync] * 4, w_plane_raw, w_scales[0])
+        nc.sync.dma_start(out=wb_raw[:].bitcast(I32), in_=wb_words[0].bitcast(I32))
+        load_scale_rows([nc.sync] * 4, wb_plane_raw, wb_scales[0])
+        nc.gpsimd.dma_start(out=rw_sb[:], in_=rw.rearrange("o (q i) -> (o q) i", i=SET))
+        with nc.allow_non_contiguous_dma(reason="one weight a partition"):
+            nc.gpsimd.dma_start(out=qw_sb[:], in_=qw.rearrange("o q -> q o"))
+
+        ident = sb.tile([P, P], F32, name="ident")
+        make_identity(nc, ident[:])
+        cw_rows = sb.tile([P, SET], F32, name="cw_rows")
+        nc.gpsimd.memset(cw_rows[Q:P, :], 0.0)
+        nc.gpsimd.tensor_scalar(out=cw_rows[0:Q, :], in0=rw_sb[:], scalar1=qw_sb[:, 0:1], scalar2=0.0, op0=ALU.mult, op1=ALU.add)
+
+        g_plane = sb.tile([P, J], U8, name="g_plane", align_bytes=64)
+        g_words = sb.tile([P, J], U32, name="g_words", align_bytes=64)
+        w_dealt = sb.tile([P, R], U32, name="w_dealt", align_bytes=64)
+        w_plane = sb.tile([P, R], U8, name="w_plane", align_bytes=64)
+        wb_dealt = sb.tile([P, 2 * N], U8, name="wb_dealt", align_bytes=64)
+        wb_plane = sb.tile([P, N], U8, name="wb_plane", align_bytes=64)
+
+        deal_columns(nc, w_dealt[:], w_raw[:], 4)
+        nc.vector.tensor_copy(g_plane[:], x_plane[:].indirect(offsets[:]))
+        nc.vector.tensor_copy(g_words[:], x_words[:].indirect(offsets[:]))
+        deal_columns(nc, w_plane[:], w_plane_raw[:], 16)
+        deal_columns(nc, wb_dealt[:].bitcast(U16), wb_raw[:].bitcast(U16), 8)
+        deal_columns(nc, wb_plane[:], wb_plane_raw[:], 16)
+
+        a_sb = sb.tile([P, PACK, J], F32, name="a_sb", align_bytes=64)
+        peak = sb.tile([P, PACK], F32, name="peak")
+        for t in range(PACK):
+            a_ps = ps.tile([P, J], F32, name="a_ps%d" % t, tag="bank%d" % t)
+            cols = slice(t * P, (t + 1) * P)
+            nc.tensor.matmul_mx(
+                out=a_ps[:],
+                lhsT=w_dealt[:, cols].bitcast(E4M3),
+                lhsT_scale=w_plane[:, cols],
+                rhs=g_words[:].bitcast(E5M2),
+                rhs_scale=g_plane[:],
+                start=True,
+                stop=True,
+            )
+            nc.scalar.copy(out=a_sb[:, t, :], in_=a_ps[:])
+            nc.vector.tensor_reduce(
+                out=peak[:, t : t + 1], in_=a_sb[:, t, :], axis=AX.X, op=ALU.max, apply_absolute_value=True
+            )
+
+        cw_ps = ps.tile([P, SET, P], F32, name="cw_ps", tag="bank0")
+        for i in range(SET):
+            nc.tensor.transpose(cw_ps[:, i, :], cw_rows[:, i : i + 1].to_broadcast([P, P]), ident[:])
+        cw = sb.tile([P, SET, Q], F32, name="cw", align_bytes=64)
+        nc.scalar.copy(out=cw[:], in_=cw_ps[:, :, 0:Q])
+
+        inv_peak = sb.tile([P, PACK], F32, name="inv_peak")
+        factor = sb.tile([P, PACK], F32, name="factor")
+        nc.vector.reciprocal(out=inv_peak[:], in_=peak[:])
+        nc.vector.tensor_tensor(out=factor[:], in0=inv_peak[:], in1=us_sb[:], op=ALU.mult)
+
+        hid = [sb.tile([P, HALF, PACK], BF16, name="hid%d" % h, align_bytes=64) for h in range(2)]
+        h_words = [sb.tile([P, HALF], U32, name="h_words%d" % h, align_bytes=64) for h in range(2)]
+        h_plane = [sb.tile([P, HALF], U8, name="h_plane%d" % h, align_bytes=64) for h in range(2)]
+        for h in range(2):
+            width = HALF if h == 0 else HALF - SCALAR_SLOTS
+            nc.vector.tensor_tensor(
+                out=hid[h][:, 0:width, :].rearrange("p (c i) t -> p c t i", i=4),
+                in0=a_sb[:, :, h * HALF : h * HALF + width].rearrange("p t (c i) -> p c t i", i=4),
+                in1=factor[:].unsqueeze(1).unsqueeze(3).to_broadcast([P, width // 4, PACK, 4]),
+                op=ALU.mult,
+            )
+            if h == 1:
+                for t in range(PACK):
+                    nc.scalar.activation(
+                        out=hid[h][:, width:HALF, t],
+                        in_=a_sb[:, t, J - SCALAR_SLOTS : J],
+                        func=mybir.ActivationFunctionType.Copy,
+                        scale=factor[:, t : t + 1],
+                    )
+            nc.vector.quantize_mx(
+                out=h_words[h][:].bitcast(E5M2), scales=h_plane[h][:], in_=hid[h][:].rearrange("p j t -> p (j t)")
+            )
+
+        weighted = [sb.tile([P, 2, SET, QH * 2], F32, name="weighted%d" % h, align_bytes=64) for h in range(2)]
+        pairs = [sb.tile([P, 2, 2, QH * 2], F32, name="pairs%d" % h, align_bytes=64) for h in range(2)]
+        y_bf = sb.tile([P, Q, 2, 2], BF16, name="y_bf", align_bytes=64)
+        y = sb.tile([P, 2, 2, Q], F32, name="y", align_bytes=64)
+        for h in range(2):
+            sets = slice(h * QH, (h + 1) * QH)
+            for tp in range(2):
+                p_ps = ps.tile([P, 2, HALF], F32, name="p_ps%d%d" % (h, tp), tag="bank%d" % (4 + 2 * h + tp))
+                for u in range(2):
+                    t = 2 * tp + u
+                    nc.tensor.matmul_mx(
+                        out=p_ps[:, u, :],
+                        lhsT=wb_dealt[:, 2 * P * t : 2 * P * (t + 1)].bitcast(E2M1),
+                        lhsT_scale=wb_plane[:, P * t : P * (t + 1)],
+                        rhs=h_words[h][:].bitcast(E5M2),
+                        rhs_scale=h_plane[h][:],
+                        start=True,
+                        stop=True,
+                    )
+                nc.vector.tensor_tensor(
+                    out=weighted[h][:, tp, :, :].rearrange("p i (q u) -> p i q u", u=2),
+                    in0=p_ps[:].rearrange("p u (q i) -> p i q u", i=SET),
+                    in1=cw[:, :, sets].unsqueeze(3).to_broadcast([P, SET, QH, 2]),
+                    op=ALU.mult,
+                )
+        for h in range(2):
+            nc.vector.tensor_tensor(
+                out=pairs[h][:], in0=weighted[h][:, :, 0:2, :], in1=weighted[h][:, :, 2:4, :], op=ALU.add
+            )
+        for h in range(2):
+            nc.vector.tensor_tensor(
+                out=y_bf[:, h * QH : (h + 1) * QH, :, :],
+                in0=pairs[h][:, :, 0, :].rearrange("p tp (q u) -> p q tp u", u=2),
+                in1=pairs[h][:, :, 1, :].rearrange("p tp (q u) -> p q tp u", u=2),
+                op=ALU.add,
+            )
+        for h in range(2):
+            nc.vector.tensor_tensor(
+                out=y[:, :, :, h * QH : (h + 1) * QH].rearrange("p tp u q -> p tp q u"),
+                in0=pairs[h][:, :, 0, :].rearrange("p tp (q u) -> p tp q u", u=2),
+                in1=pairs[h][:, :, 1, :].rearrange("p tp (q u) -> p tp q u", u=2),
+                op=ALU.add,
+            )
+        y_words = sb.tile([P, Q], U32, name="y_words", align_bytes=64)
+        y_plane = sb.tile([P, Q], U8, name="y_plane", align_bytes=64)
+        nc.vector.quantize_mx(out=y_words[:].bitcast(E4M3), scales=y_plane[:], in_=y_bf[:].rearrange("p q tp u -> p (q tp u)"))
+
+        nc.sync.dma_start(out=out_0.rearrange("(p t) q -> p (t q)", t=PACK), in_=y[:].rearrange("p tp u q -> p (tp u q)"))
+        nc.scalar.dma_start(out=out_1[0].rearrange("p c t -> p (c t)").bitcast(I32), in_=y_words[:].bitcast(I32))
+        for quad in range(4):
+            queue = nc.sync if quad % 2 == 0 else nc.scalar
+            queue.dma_start(
+                out=out_2[0, 4 * quad : 4 * quad + 4, :].bitcast(I32),
+                in_=y_plane[32 * quad : 32 * quad + 4, :].bitcast(I32),
+            )

@@ -23,7 +23,7 @@ PACK = 4
 SET = J // Q
 HALF = J // 2
 QH = Q // 2
-SCALAR_SLOTS = 64
+SCALAR_SLOTS = 80
 
 
 def load_scale_rows(queues, plane, rows):
@@ -85,16 +85,16 @@ def tile_list_picked_peakscaled_groupsums_pl_kernel(
         g_plane = sb.tile([P, J], U8, name="g_plane", align_bytes=64)
         g_words = sb.tile([P, J], U32, name="g_words", align_bytes=64)
         w_dealt = sb.tile([P, R], U32, name="w_dealt", align_bytes=64)
-        w_plane = sb.tile([P, R], U8, name="w_plane", align_bytes=64)
+        w_plane = [sb.tile([P, P], U8, name="w_plane%d" % t, align_bytes=64) for t in range(PACK)]
         wb_dealt = sb.tile([P, 2 * N], U8, name="wb_dealt", align_bytes=64)
-        wb_plane = sb.tile([P, N], U8, name="wb_plane", align_bytes=64)
+        wb_plane = [sb.tile([P, N // 2], U8, name="wb_plane%d" % tp, align_bytes=64) for tp in range(2)]
 
         deal_columns(nc, w_dealt[:], w_raw[:], 4)
         nc.vector.tensor_copy(g_plane[:], x_plane[:].indirect(offsets[:]))
         nc.vector.tensor_copy(g_words[:], x_words[:].indirect(offsets[:]))
-        deal_columns(nc, w_plane[:], w_plane_raw[:], 16)
+        for t in range(PACK):
+            nc.vector.tensor_copy(out=w_plane[t][:], in_=w_plane_raw[:, t:R:PACK])
         deal_columns(nc, wb_dealt[:].bitcast(U16), wb_raw[:].bitcast(U16), 8)
-        deal_columns(nc, wb_plane[:], wb_plane_raw[:], 16)
 
         a_sb = sb.tile([P, PACK, J], F32, name="a_sb", align_bytes=64)
         peak = sb.tile([P, PACK], F32, name="peak")
@@ -104,7 +104,7 @@ def tile_list_picked_peakscaled_groupsums_pl_kernel(
             nc.tensor.matmul_mx(
                 out=a_ps[:],
                 lhsT=w_dealt[:, cols].bitcast(E4M3),
-                lhsT_scale=w_plane[:, cols],
+                lhsT_scale=w_plane[t][:],
                 rhs=g_words[:].bitcast(E5M2),
                 rhs_scale=g_plane[:],
                 start=True,
@@ -125,6 +125,12 @@ def tile_list_picked_peakscaled_groupsums_pl_kernel(
         factor = sb.tile([P, PACK], F32, name="factor")
         nc.vector.reciprocal(out=inv_peak[:], in_=peak[:])
         nc.vector.tensor_tensor(out=factor[:], in0=inv_peak[:], in1=us_sb[:], op=ALU.mult)
+
+        for tp in range(2):
+            nc.vector.tensor_copy(
+                out=wb_plane[tp][:].rearrange("p (u c i) -> p c u i", u=2, i=16),
+                in_=wb_plane_raw[:].rearrange("p (c i t) -> p c t i", t=PACK, i=16)[:, :, 2 * tp : 2 * tp + 2, :],
+            )
 
         hid = [sb.tile([P, HALF, PACK], BF16, name="hid%d" % h, align_bytes=64) for h in range(2)]
         h_words = [sb.tile([P, HALF], U32, name="h_words%d" % h, align_bytes=64) for h in range(2)]
@@ -162,7 +168,7 @@ def tile_list_picked_peakscaled_groupsums_pl_kernel(
                     nc.tensor.matmul_mx(
                         out=p_ps[:, u, :],
                         lhsT=wb_dealt[:, 2 * P * t : 2 * P * (t + 1)].bitcast(E2M1),
-                        lhsT_scale=wb_plane[:, P * t : P * (t + 1)],
+                        lhsT_scale=wb_plane[tp][:, P * u : P * (u + 1)],
                         rhs=h_words[h][:].bitcast(E5M2),
                         rhs_scale=h_plane[h][:],
                         start=True,

from contextlib import ExitStack

import concourse.mybir as mybir
from concourse.masks import make_identity

K, T, J, R, N, Q = 512, 1024, 256, 512, 512, 64
FLOPS = 2 * K * R * J + 2 * R * N * J

F32 = mybir.dt.float32
BF16 = mybir.dt.bfloat16
I32 = mybir.dt.int32
U32 = mybir.dt.uint32
U16 = mybir.dt.uint16
U8 = mybir.dt.uint8
E4M3 = mybir.dt.float8_e4m3fn_x4
E5M2 = mybir.dt.float8_e5m2_x4
E2M1 = mybir.dt.float4_e2m1fn_x4
ALU = mybir.AluOpType
AX = mybir.AxisListType

P = 128
PACK = 4
SET = J // Q
HALF = J // 2
QH = Q // 2
SCALAR_SLOTS = 80


def load_scale_rows(queues, plane, rows):
    for quad in range(4):
        queues[quad].dma_start(
            out=plane[32 * quad : 32 * quad + 4, :].bitcast(I32),
            in_=rows[4 * quad : 4 * quad + 4, :].bitcast(I32),
        )


def deal_columns(nc, dealt, raw, run):
    nc.vector.tensor_copy(
        out=dealt.rearrange("p (t c i) -> p c t i", t=PACK, i=run),
        in_=raw.rearrange("p (c i t) -> p c t i", t=PACK, i=run),
    )


def tile_list_picked_peakscaled_groupsums_pl_kernel(
    tc, xt_words, xt_scales, w_words, w_scales, us, wb_words, wb_scales, rw, qw, offs, out_0, out_1, out_2
):
    nc = tc.nc
    with ExitStack() as ctx:
        sb = ctx.enter_context(tc.tile_pool(name="sb", bufs=1))
        ps = ctx.enter_context(tc.psum_pool(name="ps", bufs=1))

        offsets = sb.tile([P, J // 16], U16, name="offsets")
        x_words = sb.tile([P, T], U32, name="x_words", align_bytes=64)
        x_plane = sb.tile([P, T], U8, name="x_plane", align_bytes=64)
        w_raw = sb.tile([P, R], U32, name="w_raw", align_bytes=64)
        w_plane_raw = sb.tile([P, R], U8, name="w_plane_raw", align_bytes=64)
        wb_raw = sb.tile([P, 2 * N], U8, name="wb_raw", align_bytes=64)
        wb_plane_raw = sb.tile([P, N], U8, name="wb_plane_raw", align_bytes=64)
        us_sb = sb.tile([P, PACK], F32, name="us_sb")
        rw_sb = sb.tile([Q, SET], F32, name="rw_sb")
        qw_sb = sb.tile([Q, 1], F32, name="qw_sb")

        nc.gpsimd.memset(x_plane[:].bitcast(I32), 0)
        nc.vector.memset(w_plane_raw[:].bitcast(I32), 0)
        nc.vector.memset(wb_plane_raw[:].bitcast(I32), 0)

        nc.sync.dma_start(offsets[:], offs)
        nc.sync.dma_start(out=us_sb[:], in_=us.rearrange("(p t) o -> p (t o)", t=PACK))
        nc.sync.dma_start(out=w_raw[:].bitcast(I32), in_=w_words[0].rearrange("p n t -> p (n t)").bitcast(I32))
        load_scale_rows([nc.sync] * 4, x_plane, xt_scales[0])
        nc.sync.dma_start(out=x_words[:].bitcast(I32), in_=xt_words[0].rearrange("p n t -> p (n t)").bitcast(I32))
        load_scale_rows([nc.sync] * 4, w_plane_raw, w_scales[0])
        nc.sync.dma_start(out=wb_raw[:].bitcast(I32), in_=wb_words[0].bitcast(I32))
        load_scale_rows([nc.sync] * 4, wb_plane_raw, wb_scales[0])
        nc.gpsimd.dma_start(out=rw_sb[:], in_=rw.rearrange("o (q i) -> (o q) i", i=SET))
        with nc.allow_non_contiguous_dma(reason="one weight a partition"):
            nc.gpsimd.dma_start(out=qw_sb[:], in_=qw.rearrange("o q -> q o"))

        ident = sb.tile([P, P], F32, name="ident")
        make_identity(nc, ident[:])
        cw_rows = sb.tile([P, SET], F32, name="cw_rows")
        nc.gpsimd.memset(cw_rows[Q:P, :], 0.0)
        nc.gpsimd.tensor_scalar(out=cw_rows[0:Q, :], in0=rw_sb[:], scalar1=qw_sb[:, 0:1], scalar2=0.0, op0=ALU.mult, op1=ALU.add)

        g_plane = sb.tile([P, J], U8, name="g_plane", align_bytes=64)
        g_words = sb.tile([P, J], U32, name="g_words", align_bytes=64)
        w_dealt = sb.tile([P, R], U32, name="w_dealt", align_bytes=64)
        w_plane = [sb.tile([P, P], U8, name="w_plane%d" % t, align_bytes=64) for t in range(PACK)]
        wb_dealt = sb.tile([P, 2 * N], U8, name="wb_dealt", align_bytes=64)
        wb_plane = [sb.tile([P, N // 2], U8, name="wb_plane%d" % tp, align_bytes=64) for tp in range(2)]

        deal_columns(nc, w_dealt[:], w_raw[:], 4)
        nc.vector.tensor_copy(g_plane[:], x_plane[:].indirect(offsets[:]))
        nc.vector.tensor_copy(g_words[:], x_words[:].indirect(offsets[:]))
        for t in range(PACK):
            nc.vector.tensor_copy(out=w_plane[t][:], in_=w_plane_raw[:, t:R:PACK])
        deal_columns(nc, wb_dealt[:].bitcast(U16), wb_raw[:].bitcast(U16), 8)

        a_sb = sb.tile([P, PACK, J], F32, name="a_sb", align_bytes=64)
        peak = sb.tile([P, PACK], F32, name="peak")
        for t in range(PACK):
            a_ps = ps.tile([P, J], F32, name="a_ps%d" % t, tag="bank%d" % t)
            cols = slice(t * P, (t + 1) * P)
            nc.tensor.matmul_mx(
                out=a_ps[:],
                lhsT=w_dealt[:, cols].bitcast(E4M3),
                lhsT_scale=w_plane[t][:],
                rhs=g_words[:].bitcast(E5M2),
                rhs_scale=g_plane[:],
                start=True,
                stop=True,
            )
            nc.scalar.copy(out=a_sb[:, t, :], in_=a_ps[:])
            nc.vector.tensor_reduce(
                out=peak[:, t : t + 1], in_=a_sb[:, t, :], axis=AX.X, op=ALU.max, apply_absolute_value=True
            )

        cw_ps = ps.tile([P, SET, P], F32, name="cw_ps", tag="bank0")
        for i in range(SET):
            nc.tensor.transpose(cw_ps[:, i, :], cw_rows[:, i : i + 1].to_broadcast([P, P]), ident[:])
        cw = sb.tile([P, SET, Q], F32, name="cw", align_bytes=64)
        nc.scalar.copy(out=cw[:], in_=cw_ps[:, :, 0:Q])

        inv_peak = sb.tile([P, PACK], F32, name="inv_peak")
        factor = sb.tile([P, PACK], F32, name="factor")
        nc.vector.reciprocal(out=inv_peak[:], in_=peak[:])
        nc.vector.tensor_tensor(out=factor[:], in0=inv_peak[:], in1=us_sb[:], op=ALU.mult)

        for tp in range(2):
            nc.vector.tensor_copy(
                out=wb_plane[tp][:].rearrange("p (u c i) -> p c u i", u=2, i=16),
                in_=wb_plane_raw[:].rearrange("p (c i t) -> p c t i", t=PACK, i=16)[:, :, 2 * tp : 2 * tp + 2, :],
            )

        hid = [sb.tile([P, HALF, PACK], BF16, name="hid%d" % h, align_bytes=64) for h in range(2)]
        h_words = [sb.tile([P, HALF], U32, name="h_words%d" % h, align_bytes=64) for h in range(2)]
        h_plane = [sb.tile([P, HALF], U8, name="h_plane%d" % h, align_bytes=64) for h in range(2)]
        for h in range(2):
            width = HALF if h == 0 else HALF - SCALAR_SLOTS
            nc.vector.tensor_tensor(
                out=hid[h][:, 0:width, :].rearrange("p (c i) t -> p c t i", i=4),
                in0=a_sb[:, :, h * HALF : h * HALF + width].rearrange("p t (c i) -> p c t i", i=4),
                in1=factor[:].unsqueeze(1).unsqueeze(3).to_broadcast([P, width // 4, PACK, 4]),
                op=ALU.mult,
            )
            if h == 1:
                for t in range(PACK):
                    nc.scalar.activation(
                        out=hid[h][:, width:HALF, t],
                        in_=a_sb[:, t, J - SCALAR_SLOTS : J],
                        func=mybir.ActivationFunctionType.Copy,
                        scale=factor[:, t : t + 1],
                    )
            nc.vector.quantize_mx(
                out=h_words[h][:].bitcast(E5M2), scales=h_plane[h][:], in_=hid[h][:].rearrange("p j t -> p (j t)")
            )

        weighted = [sb.tile([P, 2, SET, QH * 2], F32, name="weighted%d" % h, align_bytes=64) for h in range(2)]
        pairs = [sb.tile([P, 2, 2, QH * 2], F32, name="pairs%d" % h, align_bytes=64) for h in range(2)]
        y_bf = sb.tile([P, Q, 2, 2], BF16, name="y_bf", align_bytes=64)
        y = sb.tile([P, 2, 2, Q], F32, name="y", align_bytes=64)
        for h in range(2):
            sets = slice(h * QH, (h + 1) * QH)
            for tp in range(2):
                p_ps = ps.tile([P, 2, HALF], F32, name="p_ps%d%d" % (h, tp), tag="bank%d" % (4 + 2 * h + tp))
                for u in range(2):
                    t = 2 * tp + u
                    nc.tensor.matmul_mx(
                        out=p_ps[:, u, :],
                        lhsT=wb_dealt[:, 2 * P * t : 2 * P * (t + 1)].bitcast(E2M1),
                        lhsT_scale=wb_plane[tp][:, P * u : P * (u + 1)],
                        rhs=h_words[h][:].bitcast(E5M2),
                        rhs_scale=h_plane[h][:],
                        start=True,
                        stop=True,
                    )
                nc.vector.tensor_tensor(
                    out=weighted[h][:, tp, :, :].rearrange("p i (q u) -> p i q u", u=2),
                    in0=p_ps[:].rearrange("p u (q i) -> p i q u", i=SET),
                    in1=cw[:, :, sets].unsqueeze(3).to_broadcast([P, SET, QH, 2]),
                    op=ALU.mult,
                )
        for h in range(2):
            nc.vector.tensor_tensor(
                out=pairs[h][:], in0=weighted[h][:, :, 0:2, :], in1=weighted[h][:, :, 2:4, :], op=ALU.add
            )
        for h in range(2):
            nc.vector.tensor_tensor(
                out=y_bf[:, h * QH : (h + 1) * QH, :, :],
                in0=pairs[h][:, :, 0, :].rearrange("p tp (q u) -> p q tp u", u=2),
                in1=pairs[h][:, :, 1, :].rearrange("p tp (q u) -> p q tp u", u=2),
                op=ALU.add,
            )
        for h in range(2):
            nc.vector.tensor_tensor(
                out=y[:, :, :, h * QH : (h + 1) * QH].rearrange("p tp u q -> p tp q u"),
                in0=pairs[h][:, :, 0, :].rearrange("p tp (q u) -> p tp q u", u=2),
                in1=pairs[h][:, :, 1, :].rearrange("p tp (q u) -> p tp q u", u=2),
                op=ALU.add,
            )
        y_words = sb.tile([P, Q], U32, name="y_words", align_bytes=64)
        y_plane = sb.tile([P, Q], U8, name="y_plane", align_bytes=64)
        nc.vector.quantize_mx(out=y_words[:].bitcast(E4M3), scales=y_plane[:], in_=y_bf[:].rearrange("p q tp u -> p (q tp u)"))

        nc.sync.dma_start(out=out_0.rearrange("(p t) q -> p (t q)", t=PACK), in_=y[:].rearrange("p tp u q -> p (tp u q)"))
        nc.scalar.dma_start(out=out_1[0].rearrange("p c t -> p (c t)").bitcast(I32), in_=y_words[:].bitcast(I32))
        for quad in range(4):
            queue = nc.sync if quad % 2 == 0 else nc.scalar
            queue.dma_start(
                out=out_2[0, 4 * quad : 4 * quad + 4, :].bitcast(I32),
                in_=y_plane[32 * quad : 32 * quad + 4, :].bitcast(I32),
            )
